import numpy as np
import ml_dtypes


def mxq(x, axis, fmt="e4m3"):
    dtype, down = {"e4m3": (ml_dtypes.float8_e4m3fn, 7), "e5m2": (ml_dtypes.float8_e5m2, 14)}[fmt]
    v = np.moveaxis(np.asarray(x, np.float32).astype(ml_dtypes.bfloat16).astype(np.float64), axis, -1)
    blocks = v.reshape(v.shape[:-1] + (-1, 32))
    amax = np.abs(blocks).max(-1, keepdims=True)
    byte = np.maximum(np.where(amax > 0, np.frexp(amax)[1] - 1 + 127, 0) - down, 1)
    scale = np.exp2(byte - 127.0)
    codes = (blocks / scale).astype(np.float32).astype(dtype).astype(np.float64)
    return np.moveaxis((codes * scale).reshape(v.shape), -1, axis)


WIDE = False


def mx_kscale(k):
    if not WIDE:
        return np.ones(k)
    levels = np.array([10, -10, 5, -5, 0])
    if k % 512:
        return np.exp2(np.random.permutation(np.resize(levels, k // 32))).repeat(32)
    a = np.empty((k // 512, 16))
    for p in range(k // 512):
        a[p, :8] = np.random.permutation(np.resize(levels, 8))
        for g in range(8):
            far = levels[np.abs(levels - a[p, g]) >= 10]
            a[p, g + 8] = far[np.random.randint(len(far))]
    return np.exp2(a.ravel()).repeat(32)


def f64(x):
    return np.asarray(x).astype(np.float64)


def striped(idx):
    return np.tile(idx.reshape(-1, 16).T, (8, 1)).astype(np.uint16)


def unstriped(offs):
    return offs[:16].T.reshape(-1).astype(np.int64)


def pack_weight(w):
    k, n = w.shape
    w = f64(np.asarray(w, np.float32).astype(ml_dtypes.bfloat16)).reshape(k // 32, 32, n)
    amax = np.abs(w).max(1)
    byte = np.clip(np.where(amax > 0, np.frexp(amax)[1] - 1 + 127 - 7, 1), 1, 254)
    scaled = (w * np.exp2(127.0 - byte)[:, None, :]).reshape(k, n).astype(np.float32)
    words = np.ascontiguousarray(scaled.reshape(k // 512, 128, 4, n).transpose(0, 1, 3, 2)).astype(ml_dtypes.float8_e4m3fn).view(np.uint8)
    return words, np.ascontiguousarray(byte.astype(np.uint8).reshape(k // 512, 16, n))


def unpack_weight(words, scales):
    g, p, n, _ = words.shape
    vals = np.ascontiguousarray(words).view(ml_dtypes.float8_e4m3fn).astype(np.float64) * np.repeat(np.exp2(scales.astype(np.float64) - 127.0), 8, axis=1)[..., None]
    return vals.transpose(0, 1, 3, 2).reshape(g * 512, n)


K, T, S, D, N, H, V, W, U = 512, 2048, 1024, 4, 128, 512, 256, 4096, 512


def setup_inputs():
    n = np.random.standard_normal
    s = mx_kscale(K)[:, None]
    u = mx_kscale(H)
    packed_xT = pack_weight(n((K, T)) * s)
    packed_eT = pack_weight(n((K, W)) * s)
    return {
        "x_words": packed_xT[0],
        "x_scales": packed_xT[1],
        "w1": (n((K, H)) / np.sqrt(K) / s).astype(np.float32),
        "e_words": packed_eT[0],
        "e_scales": packed_eT[1],
        "w2": (n((K, H)) / np.sqrt(K) / s).astype(np.float32),
        "loc": (n((H, U))).astype(np.float32),
        "unit": (np.random.uniform(0.6, 1.4, (H, 1)) * u[:, None]).astype(np.float32),
        "w3": (n((H, N)) / np.sqrt(H) / u[:, None]).astype(np.float32),
        "offs": striped(np.random.permutation(T)[:S]),
        "ngr": striped(np.random.permutation(W)[:S]),
        "win": striped(np.random.permutation(np.concatenate([np.arange(V), np.random.randint(0, V, U - V)]))),
    }


def reference(x_words, x_scales, w1, e_words, e_scales, w2, loc, unit, w3, offs, ngr, win):
    xq = unpack_weight(x_words, x_scales)[:, unstriped(offs)]
    y = mxq(f64(w1), 0, "e4m3").T @ xq
    e_ngr = unpack_weight(e_words, e_scales)[:, unstriped(ngr)]
    ye = mxq(f64(w2), 0, "e4m3").T @ e_ngr
    bh = y + ye
    pt = bh.reshape(len(bh), -1, D).max(axis=2)
    dp = bh - np.repeat(pt, D, axis=1)
    ed = np.exp(1.5 * np.tanh(dp))
    soft = ed.reshape(len(ed), -1, D).mean(axis=2)
    sc = soft[:, unstriped(win)]
    zz2 = sc * pt[:, unstriped(win)] + f64(loc)
    hid = f64(unit) * zz2
    return mxq(f64(w3), 0, "e4m3").T @ mxq(hid, 0, "e4m3")

@@ -1,0 +1,226 @@
+from contextlib import ExitStack
+
+import concourse.mybir as mybir
+from concourse.masks import make_identity
+
+K, T, S, D, N, H, V, W, U = 512, 2048, 1024, 4, 128, 512, 256, 4096, 512
+P = 128
+PACK = 4
+BANK = 512
+FLOPS = 2 * K * H * S * 2 + 2 * H * N * U
+
+F32 = mybir.dt.float32
+BF16 = mybir.dt.bfloat16
+I32 = mybir.dt.int32
+U32 = mybir.dt.uint32
+U16 = mybir.dt.uint16
+U8 = mybir.dt.uint8
+FP8X4 = mybir.dt.float8_e4m3fn_x4
+ALU = mybir.AluOpType
+ACT = mybir.ActivationFunctionType
+AX = mybir.AxisListType
+E_ROW = 4
+
+
+def tile_picked_ybltpt_lin_p_kernel(
+    tc, x_words, x_scales, w1, e_words, e_scales, w2, loc, unit, w3, offs, ngr, win, out
+):
+    nc = tc.nc
+    with ExitStack() as ctx:
+        keep = ctx.enter_context(tc.tile_pool(name="keep", bufs=1))
+        psum = ctx.enter_context(tc.psum_pool(name="psum", bufs=1))
+
+        def sb(name, shape, dtype):
+            return keep.tile(shape, dtype, name=name, align_bytes=64)
+
+        def bank(index, name):
+            return psum.tile([P, BANK], F32, name=name, tag="bank%d" % index)
+
+        offs_t = sb("offs_t", [P, S // 16], U16)
+        ngr_t = sb("ngr_t", [P, S // 16], U16)
+        win_t = sb("win_t", [P, U // 16], U16)
+        xw = sb("xw", [P, T], U32)
+        ew = sb("ew", [P, W], U32)
+        xs = sb("xs", [P, T], U8)
+        es = sb("es", [P, W], U8)
+        nc.vector.memset(xs[:].bitcast(I32), 0)
+        nc.vector.memset(es[:].bitcast(I32), 0)
+
+        unit_t = sb("unit_t", [P, PACK], F32)
+        nc.gpsimd.dma_start(out=unit_t[:], in_=unit.rearrange("(p t) o -> p (t o)", t=PACK))
+        ident = sb("ident", [P, P], F32)
+        make_identity(nc, ident[:])
+
+        nc.sync.dma_start(out=xw[:].bitcast(I32), in_=x_words[0].rearrange("p n t -> p (n t)").bitcast(I32))
+        nc.sync.dma_start(offs_t[:], offs)
+        for q in range(4):
+            nc.sync.dma_start(out=xs[32 * q : 32 * q + 4, :].bitcast(I32), in_=x_scales[0, 4 * q : 4 * q + 4, :].bitcast(I32))
+        w1_raw = sb("w1_raw", [P, PACK, H], F32)
+        nc.sync.dma_start(out=w1_raw[:], in_=w1.rearrange("(p j) c -> p j c", j=PACK))
+        nc.sync.dma_start(ngr_t[:], ngr)
+        for q in range(4):
+            nc.sync.dma_start(
+                out=es[32 * q + E_ROW : 32 * q + E_ROW + 4, :].bitcast(I32), in_=e_scales[0, 4 * q : 4 * q + 4, :].bitcast(I32)
+            )
+        nc.sync.dma_start(out=ew[:].bitcast(I32), in_=e_words[0].rearrange("p n t -> p (n t)").bitcast(I32))
+        w2_raw = []
+        for a in range(2):
+            w2_raw.append(sb("w2_raw%d" % a, [P, PACK, H // 2], F32))
+            nc.sync.dma_start(
+                out=w2_raw[a][:], in_=w2.rearrange("(p j) c -> p j c", j=PACK)[:, :, a * (H // 2) : (a + 1) * (H // 2)]
+            )
+        w3_raw = sb("w3_raw", [P, PACK, N], F32)
+        nc.sync.dma_start(out=w3_raw[:], in_=w3.rearrange("(p j) n -> p j n", j=PACK))
+        nc.sync.dma_start(win_t[:], win)
+        loc_raw = []
+        for t in range(PACK):
+            loc_raw.append(sb("loc_raw%d" % t, [P, U], F32))
+            nc.sync.dma_start(out=loc_raw[t][:], in_=loc.rearrange("(p t) r -> p t r", t=PACK)[:, t, :])
+
+        unit_q = sb("unit_q", [P, PACK], F32)
+        nc.scalar.activation(out=unit_q[:], in_=unit_t[:], func=ACT.Copy, scale=1.0 / D)
+
+        xs_g = sb("xs_g", [P, S], U8)
+        es_g = sb("es_g", [P, S], U8)
+        xw_g = sb("xw_g", [P, S], U32)
+        ew_g = sb("ew_g", [P, S], U32)
+        nc.vector.tensor_copy(xw_g[:], xw[:].indirect(offs_t[:]))
+        nc.vector.tensor_copy(xs_g[:], xs[:].indirect(offs_t[:]))
+        nc.vector.tensor_copy(es_g[:], es[:].indirect(ngr_t[:]))
+
+        grouped = {name: sb(name + "_grouped", [P, PACK, P, PACK], BF16) for name in ("w1", "w2")}
+
+        def cast(name, m0, m1, src, copy):
+            copy(
+                out=grouped[name][:, :, m0:m1, :].rearrange("p t m j -> p m j t"),
+                in_=src.rearrange("p j (m t) -> p m j t", t=PACK),
+            )
+
+        cast("w1", 0, P, w1_raw[:], nc.scalar.copy)
+        w1_codes = sb("w1_codes", [P, H], U32)
+        w1_sc = sb("w1_sc", [P, H], U8)
+        nc.vector.quantize_mx(out=w1_codes[:].bitcast(FP8X4), scales=w1_sc[:], in_=grouped["w1"][:].rearrange("p t m j -> p (t m j)"))
+        nc.vector.tensor_copy(ew_g[:], ew[:].indirect(ngr_t[:]))
+        cast("w2", 0, 64, w2_raw[0][:], nc.scalar.copy)
+        cast("w2", 64, 96, w2_raw[1][:, :, 0:128], nc.scalar.copy)
+        cast("w2", 96, 128, w2_raw[1][:, :, 128:256], nc.vector.tensor_copy)
+        w2_codes, w2_sc = [], []
+        for t in range(PACK):
+            w2_codes.append(sb("w2_codes%d" % t, [P, P], U32))
+            w2_sc.append(sb("w2_sc%d" % t, [P, P], U8))
+            nc.vector.quantize_mx(
+                out=w2_codes[t][:].bitcast(FP8X4), scales=w2_sc[t][:], in_=grouped["w2"][:, t, :, :].rearrange("p m j -> p (m j)")
+            )
+
+        units = [(t, h) for t in range(PACK) for h in range(2)]
+        bh = {}
+        for t, h in units:
+            bh[t, h] = bank(2 * t + h, "bh%d%d" % (t, h))
+            cols = slice(h * BANK, (h + 1) * BANK)
+            nc.tensor.matmul_mx(
+                out=bh[t, h][:],
+                lhsT=w1_codes[:, t * P : (t + 1) * P].bitcast(FP8X4),
+                lhsT_scale=w1_sc[:, t * P : (t + 1) * P],
+                rhs=xw_g[:, cols].bitcast(FP8X4),
+                rhs_scale=xs_g[:, cols],
+                start=True,
+                stop=False,
+            )
+        for t, h in units:
+            cols = slice(h * BANK, (h + 1) * BANK)
+            nc.tensor.matmul_mx(
+                out=bh[t, h][:],
+                lhsT=w2_codes[t][:].bitcast(FP8X4),
+                lhsT_scale=w2_sc[t][:],
+                rhs=ew_g[:, cols].bitcast(FP8X4),
+                rhs_scale=es_g[E_ROW:P, cols],
+                start=False,
+                stop=True,
+            )
+
+        loc_u = []
+        for t in range(PACK):
+            loc_u.append(sb("loc_u%d" % t, [P, U], F32))
+            nc.gpsimd.tensor_scalar(loc_u[t][:], loc_raw[t][:], unit_t[:, t : t + 1], 0.0, ALU.mult, ALU.add)
+
+        w3_grouped = sb("w3_grouped", [P, N, PACK], BF16)
+        w3_codes = sb("w3_codes", [P, N], U32)
+        w3_sc = sb("w3_sc", [P, N], U8)
+
+        window = [sb("window%d" % t, [P, 2 * V], F32) for t in range(PACK)]
+        hid = [sb("hid%d" % c, [P, PACK, U // 2], F32) for c in range(2)]
+        ed = {}
+
+        def max_and_diff(t):
+            dp = {}
+            for h in range(2):
+                nc.vector.tensor_reduce(
+                    out=window[t][:, V + h * P : V + (h + 1) * P], in_=bh[t, h][:].rearrange("p (v d) -> p v d", d=D), axis=AX.X, op=ALU.max
+                )
+            for h in range(2):
+                dp[h] = sb("dp%d%d" % (t, h), [P, D, P], F32)
+                nc.vector.tensor_tensor(
+                    dp[h][:],
+                    bh[t, h][:].rearrange("p (v d) -> p d v", d=D),
+                    window[t][:, V + h * P : V + (h + 1) * P].unsqueeze(1).to_broadcast([P, D, P]),
+                    ALU.subtract,
+                )
+            for h in range(2):
+                th = sb("th%d%d" % (t, h), [P, D, P], F32)
+                ed[t, h] = sb("ed%d%d" % (t, h), [P, D, P], F32)
+                nc.scalar.activation(out=th[:], in_=dp[h][:], func=ACT.Tanh)
+                nc.scalar.activation(out=ed[t, h][:], in_=th[:], func=ACT.Exp, scale=1.5)
+
+        back = {}
+
+        def sum_patch(t):
+            turned = {}
+            for h in range(2):
+                acc = bank(2 * t + h, "acc%d%d" % (t, h))
+                for d in range(D):
+                    nc.tensor.matmul(acc[:, 0:P], ed[t, h][:, d, :], ident[:], start=(d == 0), stop=(d == D - 1), is_transpose=True)
+                turned[h] = sb("turned%d%d" % (t, h), [P, P], F32)
+                nc.scalar.copy(out=turned[h][:], in_=acc[:, 0:P])
+            back[t] = bank(2 * t, "back%d" % t)
+            for h in range(2):
+                nc.tensor.transpose(back[t][:, h * P : (h + 1) * P], turned[h][:], ident[:])
+
+        def fetch(t):
+            nc.vector.scalar_tensor_tensor(window[t][:, 0:V], back[t][:, 0:V], unit_q[:, t : t + 1], window[t][:, V : 2 * V], ALU.mult, ALU.mult)
+            for c in range(2):
+                nc.vector.tensor_tensor(
+                    hid[c][:, t, :], window[t][:].indirect(win_t[:, c * 16 : (c + 1) * 16]), loc_u[t][:, c * V : (c + 1) * V], ALU.add
+                )
+
+        nc.scalar.copy(out=w3_grouped[:], in_=w3_raw[:].rearrange("p j n -> p n j"))
+        for t in range(PACK):
+            max_and_diff(t)
+            sum_patch(t)
+        nc.vector.quantize_mx(out=w3_codes[:].bitcast(FP8X4), scales=w3_sc[:], in_=w3_grouped[:].rearrange("p n j -> p (n j)"))
+        for t in range(PACK):
+            fetch(t)
+
+        hid_g, hid_codes, hid_sc = [], [], []
+        for c, copy in enumerate((nc.scalar.copy, nc.vector.tensor_copy)):
+            hid_g.append(sb("hid_g%d" % c, [P, U // 2, PACK], BF16))
+            copy(
+                out=hid_g[c][:].rearrange("p (r i) t -> p r t i", i=4),
+                in_=hid[c][:].rearrange("p t (r i) -> p r t i", i=4),
+            )
+        for c in (1, 0):
+            codes = sb("hid_codes%d" % c, [P, U // 2], U32)
+            sc = sb("hid_sc%d" % c, [P, U // 2], U8)
+            nc.vector.quantize_mx(out=codes[:].bitcast(FP8X4), scales=sc[:], in_=hid_g[c][:].rearrange("p r t -> p (r t)"))
+            res = bank(c, "res%d" % c)
+            nc.tensor.matmul_mx(
+                out=res[:, 0 : U // 2],
+                lhsT=w3_codes[:].bitcast(FP8X4),
+                lhsT_scale=w3_sc[:],
+                rhs=codes[:].bitcast(FP8X4),
+                rhs_scale=sc[:],
+                start=True,
+                stop=True,
+            )
+            staged = sb("staged%d" % c, [P, U // 2], F32)
+            (nc.scalar.copy if c == 1 else nc.vector.tensor_copy)(out=staged[:], in_=res[:, 0 : U // 2])
+            nc.sync.dma_start(out=out[:, c * (U // 2) : (c + 1) * (U // 2)], in_=staged[:])

@@ -53,15 +53,13 @@ def tile_picked_ybltpt_lin_p_kernel(
 
         nc.sync.dma_start(out=xw[:].bitcast(I32), in_=x_words[0].rearrange("p n t -> p (n t)").bitcast(I32))
         nc.sync.dma_start(offs_t[:], offs)
-        for q in range(4):
-            nc.sync.dma_start(out=xs[32 * q : 32 * q + 4, :].bitcast(I32), in_=x_scales[0, 4 * q : 4 * q + 4, :].bitcast(I32))
+        for r in range(4):
+            nc.sync.dma_start(out=xs[r:P:32, :].bitcast(I32), in_=x_scales[0, r:16:4, :].bitcast(I32))
         w1_raw = sb("w1_raw", [P, PACK, H], F32)
         nc.sync.dma_start(out=w1_raw[:], in_=w1.rearrange("(p j) c -> p j c", j=PACK))
         nc.sync.dma_start(ngr_t[:], ngr)
-        for q in range(4):
-            nc.sync.dma_start(
-                out=es[32 * q + E_ROW : 32 * q + E_ROW + 4, :].bitcast(I32), in_=e_scales[0, 4 * q : 4 * q + 4, :].bitcast(I32)
-            )
+        for r in range(4):
+            nc.sync.dma_start(out=es[E_ROW + r : P : 32, :].bitcast(I32), in_=e_scales[0, r:16:4, :].bitcast(I32))
         nc.sync.dma_start(out=ew[:].bitcast(I32), in_=e_words[0].rearrange("p n t -> p (n t)").bitcast(I32))
         w2_raw = []
         for a in range(2):
@@ -102,8 +100,8 @@ def tile_picked_ybltpt_lin_p_kernel(
         nc.vector.quantize_mx(out=w1_codes[:].bitcast(FP8X4), scales=w1_sc[:], in_=grouped["w1"][:].rearrange("p t m j -> p (t m j)"))
         nc.vector.tensor_copy(ew_g[:], ew[:].indirect(ngr_t[:]))
         cast("w2", 0, 64, w2_raw[0][:], nc.scalar.copy)
-        cast("w2", 64, 96, w2_raw[1][:, :, 0:128], nc.scalar.copy)
-        cast("w2", 96, 128, w2_raw[1][:, :, 128:256], nc.vector.tensor_copy)
+        cast("w2", 64, 84, w2_raw[1][:, :, 0:80], nc.scalar.copy)
+        cast("w2", 84, 128, w2_raw[1][:, :, 80:256], nc.vector.tensor_copy)
         w2_codes, w2_sc = [], []
         for t in range(PACK):
             w2_codes.append(sb("w2_codes%d" % t, [P, P], U32))
@@ -138,17 +136,23 @@ def tile_picked_ybltpt_lin_p_kernel(
                 stop=True,
             )
 
-        loc_u = []
+        hid = [sb("hid%d" % c, [P, PACK, U // 2], F32) for c in range(2)]
+        loc_u = {}
         for t in range(PACK):
-            loc_u.append(sb("loc_u%d" % t, [P, U], F32))
-            nc.gpsimd.tensor_scalar(loc_u[t][:], loc_raw[t][:], unit_t[:, t : t + 1], 0.0, ALU.mult, ALU.add)
+            whole = sb("loc_u%d" % t, [P, U], F32)
+            loc_u[t, 0], loc_u[t, 1] = whole[:, 0:V], whole[:, V:U]
+            if t < PACK - 1:
+                nc.gpsimd.tensor_scalar(whole[:], loc_raw[t][:], unit_t[:, t : t + 1], 0.0, ALU.mult, ALU.add)
+            else:
+                loc_u[t, 0] = hid[1][:, t - 1, :]
+                for c in range(2):
+                    nc.gpsimd.tensor_scalar(loc_u[t, c], loc_raw[t][:, c * V : (c + 1) * V], unit_t[:, t : t + 1], 0.0, ALU.mult, ALU.add)
 
         w3_grouped = sb("w3_grouped", [P, N, PACK], BF16)
         w3_codes = sb("w3_codes", [P, N], U32)
         w3_sc = sb("w3_sc", [P, N], U8)
 
         window = [sb("window%d" % t, [P, 2 * V], F32) for t in range(PACK)]
-        hid = [sb("hid%d" % c, [P, PACK, U // 2], F32) for c in range(2)]
         ed = {}
 
         def max_and_diff(t):
@@ -185,29 +189,42 @@ def tile_picked_ybltpt_lin_p_kernel(
             for h in range(2):
                 nc.tensor.transpose(back[t][:, h * P : (h + 1) * P], turned[h][:], ident[:])
 
-        def fetch(t):
+        def combine(t):
             nc.vector.scalar_tensor_tensor(window[t][:, 0:V], back[t][:, 0:V], unit_q[:, t : t + 1], window[t][:, V : 2 * V], ALU.mult, ALU.mult)
-            for c in range(2):
-                nc.vector.tensor_tensor(
-                    hid[c][:, t, :], window[t][:].indirect(win_t[:, c * 16 : (c + 1) * 16]), loc_u[t][:, c * V : (c + 1) * V], ALU.add
-                )
+
+        def fetch(t, c):
+            nc.vector.tensor_tensor(hid[c][:, t, :], window[t][:].indirect(win_t[:, c * 16 : (c + 1) * 16]), loc_u[t, c], ALU.add)
 
         nc.scalar.copy(out=w3_grouped[:], in_=w3_raw[:].rearrange("p j n -> p n j"))
         for t in range(PACK):
             max_and_diff(t)
             sum_patch(t)
+        combine(0)
+        combine(1)
+        fetch(0, 0)
+        fetch(0, 1)
+        combine(2)
+        fetch(1, 0)
+        fetch(1, 1)
+        combine(3)
+        fetch(2, 0)
+        fetch(3, 0)
+        fetch(2, 1)
+        fetch(3, 1)
         nc.vector.quantize_mx(out=w3_codes[:].bitcast(FP8X4), scales=w3_sc[:], in_=w3_grouped[:].rearrange("p n j -> p (n j)"))
-        for t in range(PACK):
-            fetch(t)
 
-        hid_g, hid_codes, hid_sc = [], [], []
-        for c, copy in enumerate((nc.scalar.copy, nc.vector.tensor_copy)):
-            hid_g.append(sb("hid_g%d" % c, [P, U // 2, PACK], BF16))
+        hid_g = [sb("hid_g%d" % c, [P, U // 2, PACK], BF16) for c in range(2)]
+
+        def weave(c, r0, r1, copy):
             copy(
-                out=hid_g[c][:].rearrange("p (r i) t -> p r t i", i=4),
-                in_=hid[c][:].rearrange("p t (r i) -> p r t i", i=4),
+                out=hid_g[c][:, r0:r1, :].rearrange("p (r i) t -> p r t i", i=4),
+                in_=hid[c][:, :, r0:r1].rearrange("p t (r i) -> p r t i", i=4),
             )
-        for c in (1, 0):
+
+        weave(0, 0, V, nc.scalar.copy)
+        weave(1, 0, 96, nc.scalar.copy)
+        weave(1, 96, V, nc.vector.tensor_copy)
+        for c in range(2):
             codes = sb("hid_codes%d" % c, [P, U // 2], U32)
             sc = sb("hid_sc%d" % c, [P, U // 2], U8)
             nc.vector.quantize_mx(out=codes[:].bitcast(FP8X4), scales=sc[:], in_=hid_g[c][:].rearrange("p r t -> p (r t)"))
@@ -222,5 +239,5 @@ def tile_picked_ybltpt_lin_p_kernel(
                 stop=True,
             )
             staged = sb("staged%d" % c, [P, U // 2], F32)
-            (nc.scalar.copy if c == 1 else nc.vector.tensor_copy)(out=staged[:], in_=res[:, 0 : U // 2])
+            nc.scalar.copy(out=staged[:], in_=res[:, 0 : U // 2])
             nc.sync.dma_start(out=out[:, c * (U // 2) : (c + 1) * (U // 2)], in_=staged[:])

@@ -47,7 +47,6 @@ def tile_picked_ybltpt_lin_p_kernel(
         nc.vector.memset(es[:].bitcast(I32), 0)
 
         unit_t = sb("unit_t", [P, PACK], F32)
-        nc.gpsimd.dma_start(out=unit_t[:], in_=unit.rearrange("(p t) o -> p (t o)", t=PACK))
         ident = sb("ident", [P, P], F32)
         make_identity(nc, ident[:])
 
@@ -68,15 +67,18 @@ def tile_picked_ybltpt_lin_p_kernel(
                 out=w2_raw[a][:], in_=w2.rearrange("(p j) c -> p j c", j=PACK)[:, :, a * (H // 2) : (a + 1) * (H // 2)]
             )
         w3_raw = sb("w3_raw", [P, PACK, N], F32)
-        nc.sync.dma_start(out=w3_raw[:], in_=w3.rearrange("(p j) n -> p j n", j=PACK))
+        for q in range(2):
+            nc.sync.dma_start(out=w3_raw[q:P:2, :, :], in_=w3.rearrange("(g t q) n -> q g t n", t=PACK, q=2)[q])
+        for q in range(2):
+            nc.sync.dma_start(out=unit_t[q:P:2, :], in_=unit.rearrange("(g t q) o -> q g (t o)", t=PACK, q=2)[q])
         nc.sync.dma_start(win_t[:], win)
         loc_raw = []
         for t in range(PACK):
             loc_raw.append(sb("loc_raw%d" % t, [P, U], F32))
-            nc.sync.dma_start(out=loc_raw[t][:], in_=loc.rearrange("(p t) r -> p t r", t=PACK)[:, t, :])
+            nc.sync.dma_start(out=loc_raw[t][:], in_=loc.rearrange("(g t q) r -> t g q r", t=PACK, q=2)[t])
 
         unit_q = sb("unit_q", [P, PACK], F32)
-        nc.scalar.activation(out=unit_q[:], in_=unit_t[:], func=ACT.Copy, scale=1.0 / D)
+        nc.gpsimd.tensor_scalar(unit_q[:], unit_t[:], 1.0 / D, 0.0, ALU.mult, ALU.add)
 
         xs_g = sb("xs_g", [P, S], U8)
         es_g = sb("es_g", [P, S], U8)
@@ -90,11 +92,16 @@ def tile_picked_ybltpt_lin_p_kernel(
 
         def cast(name, m0, m1, src, copy):
             copy(
-                out=grouped[name][:, :, m0:m1, :].rearrange("p t m j -> p m j t"),
-                in_=src.rearrange("p j (m t) -> p m j t", t=PACK),
+                out=grouped[name][:, :, m0:m1, :].rearrange("p t (g q) j -> p g t j q", q=2),
+                in_=src.rearrange("p j (g t q) -> p g t j q", t=PACK, q=2),
             )
 
-        cast("w1", 0, P, w1_raw[:], nc.scalar.copy)
+        for t in range(PACK):
+            nc.scalar.activation(
+                out=grouped["w1"][:, t, :, :].rearrange("p (g q) j -> p g j q", q=2),
+                in_=w1_raw[:].rearrange("p j (g t q) -> p t g j q", t=PACK, q=2)[:, t],
+                func=ACT.Copy,
+            )
         w1_codes = sb("w1_codes", [P, H], U32)
         w1_sc = sb("w1_sc", [P, H], U8)
         nc.vector.quantize_mx(out=w1_codes[:].bitcast(FP8X4), scales=w1_sc[:], in_=grouped["w1"][:].rearrange("p t m j -> p (t m j)"))
@@ -195,7 +202,7 @@ def tile_picked_ybltpt_lin_p_kernel(
         def fetch(t, c):
             nc.vector.tensor_tensor(hid[c][:, t, :], window[t][:].indirect(win_t[:, c * 16 : (c + 1) * 16]), loc_u[t, c], ALU.add)
 
-        nc.scalar.copy(out=w3_grouped[:], in_=w3_raw[:].rearrange("p j n -> p n j"))
+        nc.scalar.copy(out=w3_grouped[:].rearrange("p (n i) j -> p n j i", i=2), in_=w3_raw[:].rearrange("p j (n i) -> p n j i", i=2))
         for t in range(PACK):
             max_and_diff(t)
             sum_patch(t)
@@ -217,8 +224,8 @@ def tile_picked_ybltpt_lin_p_kernel(
 
         def weave(c, r0, r1, copy):
             copy(
-                out=hid_g[c][:, r0:r1, :].rearrange("p (r i) t -> p r t i", i=4),
-                in_=hid[c][:, :, r0:r1].rearrange("p t (r i) -> p r t i", i=4),
+                out=hid_g[c][:, r0:r1, :].rearrange("p (r i) t -> p r t i", i=2),
+                in_=hid[c][:, :, r0:r1].rearrange("p t (r i) -> p r t i", i=2),
             )
 
         weave(0, 0, V, nc.scalar.copy)

from contextlib import ExitStack

import concourse.mybir as mybir
from concourse.masks import make_identity

K, T, S, D, N, H, V, W, U = 512, 2048, 1024, 4, 128, 512, 256, 4096, 512
P = 128
PACK = 4
BANK = 512
FLOPS = 2 * K * H * S * 2 + 2 * H * N * U

F32 = mybir.dt.float32
BF16 = mybir.dt.bfloat16
I32 = mybir.dt.int32
U32 = mybir.dt.uint32
U16 = mybir.dt.uint16
U8 = mybir.dt.uint8
FP8X4 = mybir.dt.float8_e4m3fn_x4
ALU = mybir.AluOpType
ACT = mybir.ActivationFunctionType
AX = mybir.AxisListType
E_ROW = 4


def tile_picked_ybltpt_lin_p_kernel(
    tc, x_words, x_scales, w1, e_words, e_scales, w2, loc, unit, w3, offs, ngr, win, out
):
    nc = tc.nc
    with ExitStack() as ctx:
        keep = ctx.enter_context(tc.tile_pool(name="keep", bufs=1))
        psum = ctx.enter_context(tc.psum_pool(name="psum", bufs=1))

        def sb(name, shape, dtype):
            return keep.tile(shape, dtype, name=name, align_bytes=64)

        def bank(index, name):
            return psum.tile([P, BANK], F32, name=name, tag="bank%d" % index)

        offs_t = sb("offs_t", [P, S // 16], U16)
        ngr_t = sb("ngr_t", [P, S // 16], U16)
        win_t = sb("win_t", [P, U // 16], U16)
        xw = sb("xw", [P, T], U32)
        ew = sb("ew", [P, W], U32)
        xs = sb("xs", [P, T], U8)
        es = sb("es", [P, W], U8)
        nc.vector.memset(xs[:].bitcast(I32), 0)
        nc.vector.memset(es[:].bitcast(I32), 0)

        unit_t = sb("unit_t", [P, PACK], F32)
        ident = sb("ident", [P, P], F32)
        make_identity(nc, ident[:])

        nc.sync.dma_start(out=xw[:].bitcast(I32), in_=x_words[0].rearrange("p n t -> p (n t)").bitcast(I32))
        nc.sync.dma_start(offs_t[:], offs)
        for r in range(4):
            nc.sync.dma_start(out=xs[r:P:32, :].bitcast(I32), in_=x_scales[0, r:16:4, :].bitcast(I32))
        w1_raw = sb("w1_raw", [P, PACK, H], F32)
        nc.sync.dma_start(out=w1_raw[:], in_=w1.rearrange("(p j) c -> p j c", j=PACK))
        nc.sync.dma_start(ngr_t[:], ngr)
        for r in range(4):
            nc.sync.dma_start(out=es[E_ROW + r : P : 32, :].bitcast(I32), in_=e_scales[0, r:16:4, :].bitcast(I32))
        nc.sync.dma_start(out=ew[:].bitcast(I32), in_=e_words[0].rearrange("p n t -> p (n t)").bitcast(I32))
        w2_raw = []
        for a in range(2):
            w2_raw.append(sb("w2_raw%d" % a, [P, PACK, H // 2], F32))
            nc.sync.dma_start(
                out=w2_raw[a][:], in_=w2.rearrange("(p j) c -> p j c", j=PACK)[:, :, a * (H // 2) : (a + 1) * (H // 2)]
            )
        w3_raw = sb("w3_raw", [P, PACK, N], F32)
        for q in range(2):
            nc.sync.dma_start(out=w3_raw[q:P:2, :, :], in_=w3.rearrange("(g t q) n -> q g t n", t=PACK, q=2)[q])
        for q in range(2):
            nc.sync.dma_start(out=unit_t[q:P:2, :], in_=unit.rearrange("(g t q) o -> q g (t o)", t=PACK, q=2)[q])
        nc.sync.dma_start(win_t[:], win)
        loc_raw = []
        for t in range(PACK):
            loc_raw.append(sb("loc_raw%d" % t, [P, U], F32))
            nc.sync.dma_start(out=loc_raw[t][:], in_=loc.rearrange("(g t q) r -> t g q r", t=PACK, q=2)[t])

        unit_q = sb("unit_q", [P, PACK], F32)
        nc.gpsimd.tensor_scalar(unit_q[:], unit_t[:], 1.0 / D, 0.0, ALU.mult, ALU.add)

        xs_g = sb("xs_g", [P, S], U8)
        es_g = sb("es_g", [P, S], U8)
        xw_g = sb("xw_g", [P, S], U32)
        ew_g = sb("ew_g", [P, S], U32)
        nc.vector.tensor_copy(xw_g[:], xw[:].indirect(offs_t[:]))
        nc.vector.tensor_copy(xs_g[:], xs[:].indirect(offs_t[:]))
        nc.vector.tensor_copy(es_g[:], es[:].indirect(ngr_t[:]))

        grouped = {name: sb(name + "_grouped", [P, PACK, P, PACK], BF16) for name in ("w1", "w2")}

        def cast(name, m0, m1, src, copy):
            copy(
                out=grouped[name][:, :, m0:m1, :].rearrange("p t (g q) j -> p g t j q", q=2),
                in_=src.rearrange("p j (g t q) -> p g t j q", t=PACK, q=2),
            )

        for t in range(PACK):
            nc.scalar.activation(
                out=grouped["w1"][:, t, :, :].rearrange("p (g q) j -> p g j q", q=2),
                in_=w1_raw[:].rearrange("p j (g t q) -> p t g j q", t=PACK, q=2)[:, t],
                func=ACT.Copy,
            )
        w1_codes = sb("w1_codes", [P, H], U32)
        w1_sc = sb("w1_sc", [P, H], U8)
        nc.vector.quantize_mx(out=w1_codes[:].bitcast(FP8X4), scales=w1_sc[:], in_=grouped["w1"][:].rearrange("p t m j -> p (t m j)"))
        nc.vector.tensor_copy(ew_g[:], ew[:].indirect(ngr_t[:]))
        cast("w2", 0, 64, w2_raw[0][:], nc.scalar.copy)
        cast("w2", 64, 84, w2_raw[1][:, :, 0:80], nc.scalar.copy)
        cast("w2", 84, 128, w2_raw[1][:, :, 80:256], nc.vector.tensor_copy)
        w2_codes, w2_sc = [], []
        for t in range(PACK):
            w2_codes.append(sb("w2_codes%d" % t, [P, P], U32))
            w2_sc.append(sb("w2_sc%d" % t, [P, P], U8))
            nc.vector.quantize_mx(
                out=w2_codes[t][:].bitcast(FP8X4), scales=w2_sc[t][:], in_=grouped["w2"][:, t, :, :].rearrange("p m j -> p (m j)")
            )

        units = [(t, h) for t in range(PACK) for h in range(2)]
        bh = {}
        for t, h in units:
            bh[t, h] = bank(2 * t + h, "bh%d%d" % (t, h))
            cols = slice(h * BANK, (h + 1) * BANK)
            nc.tensor.matmul_mx(
                out=bh[t, h][:],
                lhsT=w1_codes[:, t * P : (t + 1) * P].bitcast(FP8X4),
                lhsT_scale=w1_sc[:, t * P : (t + 1) * P],
                rhs=xw_g[:, cols].bitcast(FP8X4),
                rhs_scale=xs_g[:, cols],
                start=True,
                stop=False,
            )
        for t, h in units:
            cols = slice(h * BANK, (h + 1) * BANK)
            nc.tensor.matmul_mx(
                out=bh[t, h][:],
                lhsT=w2_codes[t][:].bitcast(FP8X4),
                lhsT_scale=w2_sc[t][:],
                rhs=ew_g[:, cols].bitcast(FP8X4),
                rhs_scale=es_g[E_ROW:P, cols],
                start=False,
                stop=True,
            )

        hid = [sb("hid%d" % c, [P, PACK, U // 2], F32) for c in range(2)]
        loc_u = {}
        for t in range(PACK):
            whole = sb("loc_u%d" % t, [P, U], F32)
            loc_u[t, 0], loc_u[t, 1] = whole[:, 0:V], whole[:, V:U]
            if t < PACK - 1:
                nc.gpsimd.tensor_scalar(whole[:], loc_raw[t][:], unit_t[:, t : t + 1], 0.0, ALU.mult, ALU.add)
            else:
                loc_u[t, 0] = hid[1][:, t - 1, :]
                for c in range(2):
                    nc.gpsimd.tensor_scalar(loc_u[t, c], loc_raw[t][:, c * V : (c + 1) * V], unit_t[:, t : t + 1], 0.0, ALU.mult, ALU.add)

        w3_grouped = sb("w3_grouped", [P, N, PACK], BF16)
        w3_codes = sb("w3_codes", [P, N], U32)
        w3_sc = sb("w3_sc", [P, N], U8)

        window = [sb("window%d" % t, [P, 2 * V], F32) for t in range(PACK)]
        ed = {}

        def max_and_diff(t):
            dp = {}
            for h in range(2):
                nc.vector.tensor_reduce(
                    out=window[t][:, V + h * P : V + (h + 1) * P], in_=bh[t, h][:].rearrange("p (v d) -> p v d", d=D), axis=AX.X, op=ALU.max
                )
            for h in range(2):
                dp[h] = sb("dp%d%d" % (t, h), [P, D, P], F32)
                nc.vector.tensor_tensor(
                    dp[h][:],
                    bh[t, h][:].rearrange("p (v d) -> p d v", d=D),
                    window[t][:, V + h * P : V + (h + 1) * P].unsqueeze(1).to_broadcast([P, D, P]),
                    ALU.subtract,
                )
            for h in range(2):
                th = sb("th%d%d" % (t, h), [P, D, P], F32)
                ed[t, h] = sb("ed%d%d" % (t, h), [P, D, P], F32)
                nc.scalar.activation(out=th[:], in_=dp[h][:], func=ACT.Tanh)
                nc.scalar.activation(out=ed[t, h][:], in_=th[:], func=ACT.Exp, scale=1.5)

        back = {}

        def sum_patch(t):
            turned = {}
            for h in range(2):
                acc = bank(2 * t + h, "acc%d%d" % (t, h))
                for d in range(D):
                    nc.tensor.matmul(acc[:, 0:P], ed[t, h][:, d, :], ident[:], start=(d == 0), stop=(d == D - 1), is_transpose=True)
                turned[h] = sb("turned%d%d" % (t, h), [P, P], F32)
                nc.scalar.copy(out=turned[h][:], in_=acc[:, 0:P])
            back[t] = bank(2 * t, "back%d" % t)
            for h in range(2):
                nc.tensor.transpose(back[t][:, h * P : (h + 1) * P], turned[h][:], ident[:])

        def combine(t):
            nc.vector.scalar_tensor_tensor(window[t][:, 0:V], back[t][:, 0:V], unit_q[:, t : t + 1], window[t][:, V : 2 * V], ALU.mult, ALU.mult)

        def fetch(t, c):
            nc.vector.tensor_tensor(hid[c][:, t, :], window[t][:].indirect(win_t[:, c * 16 : (c + 1) * 16]), loc_u[t, c], ALU.add)

        nc.scalar.copy(out=w3_grouped[:].rearrange("p (n i) j -> p n j i", i=2), in_=w3_raw[:].rearrange("p j (n i) -> p n j i", i=2))
        for t in range(PACK):
            max_and_diff(t)
            sum_patch(t)
        combine(0)
        combine(1)
        fetch(0, 0)
        fetch(0, 1)
        combine(2)
        fetch(1, 0)
        fetch(1, 1)
        combine(3)
        fetch(2, 0)
        fetch(3, 0)
        fetch(2, 1)
        fetch(3, 1)
        nc.vector.quantize_mx(out=w3_codes[:].bitcast(FP8X4), scales=w3_sc[:], in_=w3_grouped[:].rearrange("p n j -> p (n j)"))

        hid_g = [sb("hid_g%d" % c, [P, U // 2, PACK], BF16) for c in range(2)]

        def weave(c, r0, r1, copy):
            copy(
                out=hid_g[c][:, r0:r1, :].rearrange("p (r i) t -> p r t i", i=2),
                in_=hid[c][:, :, r0:r1].rearrange("p t (r i) -> p r t i", i=2),
            )

        weave(0, 0, V, nc.scalar.copy)
        weave(1, 0, 96, nc.scalar.copy)
        weave(1, 96, V, nc.vector.tensor_copy)
        for c in range(2):
            codes = sb("hid_codes%d" % c, [P, U // 2], U32)
            sc = sb("hid_sc%d" % c, [P, U // 2], U8)
            nc.vector.quantize_mx(out=codes[:].bitcast(FP8X4), scales=sc[:], in_=hid_g[c][:].rearrange("p r t -> p (r t)"))
            res = bank(c, "res%d" % c)
            nc.tensor.matmul_mx(
                out=res[:, 0 : U // 2],
                lhsT=w3_codes[:].bitcast(FP8X4),
                lhsT_scale=w3_sc[:],
                rhs=codes[:].bitcast(FP8X4),
                rhs_scale=sc[:],
                start=True,
                stop=True,
            )
            staged = sb("staged%d" % c, [P, U // 2], F32)
            nc.scalar.copy(out=staged[:], in_=res[:, 0 : U // 2])
            nc.sync.dma_start(out=out[:, c * (U // 2) : (c + 1) * (U // 2)], in_=staged[:])
